import numpy as np
import ml_dtypes


def mxq(x, axis, fmt="e4m3"):
    dtype, down = {"e4m3": (ml_dtypes.float8_e4m3fn, 7), "e5m2": (ml_dtypes.float8_e5m2, 14)}[fmt]
    v = np.moveaxis(np.asarray(x, np.float32).astype(ml_dtypes.bfloat16).astype(np.float64), axis, -1)
    blocks = v.reshape(v.shape[:-1] + (-1, 32))
    amax = np.abs(blocks).max(-1, keepdims=True)
    byte = np.maximum(np.where(amax > 0, np.frexp(amax)[1] - 1 + 127, 0) - down, 1)
    scale = np.exp2(byte - 127.0)
    codes = (blocks / scale).astype(np.float32).astype(dtype).astype(np.float64)
    return np.moveaxis((codes * scale).reshape(v.shape), -1, axis)


WIDE = False


def mx_kscale(k, group=512):
    if not WIDE:
        return np.ones(k)
    levels = np.array([18, -18])
    if group != 512:
        return np.exp2(np.random.permutation(np.resize(levels, k // group))).repeat(group)
    if k % 512:
        return np.exp2(np.random.permutation(np.resize(levels, k // 32))).repeat(32)
    a = np.empty((k // 512, 16))
    for p in range(k // 512):
        a[p, :8] = np.random.permutation(np.resize(levels, 8))
        for g in range(8):
            far = levels[np.abs(levels - a[p, g]) >= 10]
            a[p, g + 8] = far[np.random.randint(len(far))]
    return np.exp2(a.ravel()).repeat(32)


def f64(x):
    return np.asarray(x).astype(np.float64)


E2M1 = np.array([0.0, 0.5, 1.0, 1.5, 2.0, 3.0, 4.0, 6.0, -0.0, -0.5, -1.0, -1.5, -2.0, -3.0, -4.0, -6.0])


def pack_group(w):
    k, n = w.shape
    w = f64(np.asarray(w, np.float32).astype(ml_dtypes.bfloat16)).reshape(k // 32, 32, n)
    amax = np.abs(w).max(1)
    mant, ex = np.frexp(amax / 6.0)
    byte = np.clip(np.where(amax > 0, np.where(mant > 0.5, ex, ex - 1) + 127, 1), 1, 254)
    scaled = (w * np.exp2(127.0 - byte)[:, None, :]).reshape(k, n).astype(np.float32)
    c = np.ascontiguousarray(scaled.reshape(k // 4, 4, n).transpose(0, 2, 1)).astype(ml_dtypes.float4_e2m1fn).view(np.uint8) & 0xF
    return np.ascontiguousarray((c[..., 0::2] | (c[..., 1::2] << 4)).reshape(k // 4, 2 * n)), byte.astype(np.uint8)


def unpack_group(words, scales):
    p, n = words.shape[0], scales.shape[1]
    words = np.ascontiguousarray(words).reshape(p, n, 2)
    nib = np.empty((p, n, 4), np.uint8)
    nib[..., 0::2] = words & 0xF
    nib[..., 1::2] = words >> 4
    return E2M1[nib].transpose(0, 2, 1).reshape(4 * p, n) * np.repeat(np.exp2(scales.astype(np.float64) - 127.0), 32, axis=0)


G, D, M, N = 4, 128, 256, 512


def setup_inputs():
    n = np.random.standard_normal
    s = mx_kscale(D, 0)[:, None]
    w_ = [pack_group(w) for w in n((G, D, M)) / np.sqrt(D) / s]
    u_ = [pack_group(w) for w in n((G, D, M)) / np.sqrt(D) / s]
    return {
        "x": (n((G, D, N)) * s).astype(np.float32),
        "w_words": np.stack([w[0] for w in w_]),
        "w_scales": np.stack([w[1] for w in w_]),
        "u_words": np.stack([w[0] for w in u_]),
        "u_scales": np.stack([w[1] for w in u_]),
        "r": n((G, M, N)).astype(np.float32),
    }


def reference(x, w_words, w_scales, u_words, u_scales, r):
    xq = mxq(f64(x), 1, "e4m3")
    h = np.stack([unpack_group(w_words[g], w_scales[g]) for g in range(G)]).transpose(0, 2, 1) @ xq
    g = np.stack([unpack_group(u_words[g], u_scales[g]) for g in range(G)]).transpose(0, 2, 1) @ xq
    y = np.maximum(h, 0.0) * g
    y = y + f64(r)
    return y

@@ -1,0 +1,120 @@
+from contextlib import ExitStack
+
+import concourse.mybir as mybir
+
+G, D, M, N = 4, 128, 256, 512
+FLOPS = 2 * 2 * G * D * M * N
+
+F32 = mybir.dt.float32
+BF16 = mybir.dt.bfloat16
+I32 = mybir.dt.int32
+U32 = mybir.dt.uint32
+U8 = mybir.dt.uint8
+FP8X4 = mybir.dt.float8_e4m3fn_x4
+FP4X4 = mybir.dt.float4_e2m1fn_x4
+ALU = mybir.AluOpType
+ACT = mybir.ActivationFunctionType
+
+P = 128
+PACK = 4
+ROWS = D // PACK
+BLOCKS = D // 32
+M_TILE = 128
+HALVES = M // M_TILE
+X_CHUNK = 256
+V_COLS = 168
+
+
+def tile_rows_gglu_relu_res_kernel(tc, x, w_words, w_scales, u_words, u_scales, r, out):
+    nc = tc.nc
+    with ExitStack() as ctx:
+        keep = ctx.enter_context(tc.tile_pool(name="keep", bufs=1))
+        psum = ctx.enter_context(tc.psum_pool(name="psum", bufs=1))
+        ctx.enter_context(tc.manual_schedule())
+
+        chunks = N // X_CHUNK
+        x_rows = x.rearrange("g (p j) n -> (g p) j n", j=PACK)
+        x_raw = [keep.tile([P, PACK, X_CHUNK], F32, name="x_raw%d" % c) for c in range(chunks)]
+        x_bf = [keep.tile([P, X_CHUNK, PACK], BF16, name="x_bf%d" % c, align_bytes=256) for c in range(chunks)]
+        x_codes = keep.tile([P, N], U32, align_bytes=256)
+        x_scale = keep.tile([P, N], U8, align_bytes=256)
+        words = [keep.tile([P, 2 * M], U8, name="words%d" % i, align_bytes=256) for i in range(2)]
+        scales = keep.tile([P, 2, M], U8, align_bytes=256)
+        warm = keep.tile([P, 16], F32)
+        banks = [[psum.tile([M_TILE, N], F32, name="bank%d_%d" % (g, i)) for i in range(2)] for g in range(G)]
+        r_view = r.rearrange("g (h p) n -> h p g n", p=M_TILE)
+        r_sb = [[keep.tile([P, 2, N], F32, name="r%d_%d" % (h, q)) for q in range(G // 2)] for h in range(HALVES)]
+
+        nc.vector.memset(scales[:].rearrange("p a m -> p (a m)").bitcast(I32), 0)
+        nc.vector.memset(warm[:, 0:8], 0.0)
+        nc.scalar.activation(out=warm[:, 8:9], in_=warm[:, 0:1], func=ACT.Relu)
+
+        def load_scales(g):
+            for i, src in enumerate((w_scales, u_scales)):
+                nc.sync.dma_start(out=scales[ROWS * g : ROWS * g + BLOCKS, i, :].bitcast(I32), in_=src[g].bitcast(I32))
+
+        def load_r(h, q):
+            nc.sync.dma_start(out=r_sb[h][q][:], in_=r_view[h, :, 2 * q : 2 * q + 2, :])
+
+        for c in range(chunks):
+            nc.sync.dma_start(out=x_raw[c][:], in_=x_rows[:, :, c * X_CHUNK : (c + 1) * X_CHUNK])
+        for i, src in enumerate((w_words, u_words)):
+            nc.sync.dma_start(out=words[i][:].bitcast(I32), in_=src.rearrange("g p b -> (g p) b").bitcast(I32))
+        load_scales(0)
+        load_scales(1)
+        load_r(0, 0)
+        load_scales(2)
+        load_scales(3)
+        load_r(0, 1)
+        load_r(1, 0)
+        load_r(1, 1)
+
+        for c in range(chunks):
+            dst = x_bf[c][:].rearrange("p (a i) j -> p a j i", i=4)
+            src = x_raw[c][:].rearrange("p j (a i) -> p a j i", i=4)
+            nc.vector.tensor_copy(out=dst[:, : V_COLS // 4], in_=src[:, : V_COLS // 4])
+            nc.scalar.copy(out=dst[:, V_COLS // 4 :], in_=src[:, V_COLS // 4 :])
+            cols = slice(c * X_CHUNK, (c + 1) * X_CHUNK)
+            nc.vector.quantize_mx(
+                out=x_codes[:, cols].bitcast(FP8X4),
+                scales=x_scale[:, cols],
+                in_=x_bf[c][:].rearrange("p n j -> p (n j)"),
+            )
+
+        def product(g, h, i):
+            rows = slice(ROWS * g, ROWS * (g + 1))
+            nc.tensor.matmul_mx(
+                out=banks[g][i][:],
+                lhsT=words[i][rows, 2 * M_TILE * h : 2 * M_TILE * (h + 1)].bitcast(FP4X4),
+                lhsT_scale=scales[rows, i, M_TILE * h : M_TILE * (h + 1)],
+                rhs=x_codes[rows, :].bitcast(FP8X4),
+                rhs_scale=x_scale[rows, :],
+                start=True,
+                stop=True,
+            )
+
+        tiles = [(h, g) for h in range(HALVES) for g in range(G)]
+        gate = [keep.tile([P, N], F32, name="gate%d" % t) for t in range(len(tiles))]
+        prod = [keep.tile([P, N], F32, name="prod%d" % t) for t in range(len(tiles))]
+        res = [keep.tile([P, N], F32, name="res%d" % t) for t in range(len(tiles))]
+
+        def finish(t):
+            h, g = tiles[t]
+            nc.vector.tensor_tensor(out=res[t][:], in0=prod[t][:], in1=r_sb[h][g // 2][:, g % 2, :], op=ALU.add)
+            nc.sync.dma_start(out=out[g, M_TILE * h : M_TILE * (h + 1), :], in_=res[t][:])
+
+        for pair in range(G // 2):
+            for i in range(2):
+                for g in (2 * pair, 2 * pair + 1):
+                    product(g, 0, i)
+
+        for t, (h, g) in enumerate(tiles):
+            nc.scalar.activation(out=gate[t][:], in_=banks[g][0][:], func=ACT.Relu)
+            if h + 1 < HALVES:
+                product(g, h + 1, 0)
+            nc.vector.tensor_tensor(out=prod[t][:], in0=banks[g][1][:], in1=gate[t][:], op=ALU.mult)
+            if h + 1 < HALVES:
+                product(g, h + 1, 1)
+            if t > 0:
+                finish(t - 1)
+        finish(len(tiles) - 1)

@@ -23,6 +23,7 @@ M_TILE = 128
 HALVES = M // M_TILE
 X_CHUNK = 256
 V_COLS = 168
+POOL_COLS = (384, 384, 384, 128)
 
 
 def tile_rows_gglu_relu_res_kernel(tc, x, w_words, w_scales, u_words, u_scales, r, out):
@@ -40,14 +41,17 @@ def tile_rows_gglu_relu_res_kernel(tc, x, w_words, w_scales, u_words, u_scales, 
         x_scale = keep.tile([P, N], U8, align_bytes=256)
         words = [keep.tile([P, 2 * M], U8, name="words%d" % i, align_bytes=256) for i in range(2)]
         scales = keep.tile([P, 2, M], U8, align_bytes=256)
-        warm = keep.tile([P, 16], F32)
+        warm = keep.tile([P, 8], F32)
+        warm_act = keep.tile([P, 8], F32)
+        warm_pool = keep.tile([P, 8], F32)
         banks = [[psum.tile([M_TILE, N], F32, name="bank%d_%d" % (g, i)) for i in range(2)] for g in range(G)]
         r_view = r.rearrange("g (h p) n -> h p g n", p=M_TILE)
         r_sb = [[keep.tile([P, 2, N], F32, name="r%d_%d" % (h, q)) for q in range(G // 2)] for h in range(HALVES)]
 
         nc.vector.memset(scales[:].rearrange("p a m -> p (a m)").bitcast(I32), 0)
-        nc.vector.memset(warm[:, 0:8], 0.0)
-        nc.scalar.activation(out=warm[:, 8:9], in_=warm[:, 0:1], func=ACT.Relu)
+        nc.vector.memset(warm[:], 0.0)
+        nc.scalar.activation(out=warm_act[:, 0:1], in_=warm[:, 0:1], func=ACT.Relu)
+        nc.gpsimd.tensor_tensor(out=warm_pool[:], in0=warm[:], in1=warm[:], op=ALU.add)
 
         def load_scales(g):
             for i, src in enumerate((w_scales, u_scales)):
@@ -96,25 +100,38 @@ def tile_rows_gglu_relu_res_kernel(tc, x, w_words, w_scales, u_words, u_scales, 
         tiles = [(h, g) for h in range(HALVES) for g in range(G)]
         gate = [keep.tile([P, N], F32, name="gate%d" % t) for t in range(len(tiles))]
         prod = [keep.tile([P, N], F32, name="prod%d" % t) for t in range(len(tiles))]
-        res = [keep.tile([P, N], F32, name="res%d" % t) for t in range(len(tiles))]
+        res = [
+            prod[t - 1] if t % 2 == 0 and t > 0 else keep.tile([P, N], F32, name="res%d" % t) for t in range(len(tiles))
+        ]
 
-        def finish(t):
+        def add_residual(engine, t, cols):
             h, g = tiles[t]
-            nc.vector.tensor_tensor(out=res[t][:], in0=prod[t][:], in1=r_sb[h][g // 2][:, g % 2, :], op=ALU.add)
+            engine.tensor_tensor(out=res[t][:, cols], in0=prod[t][:, cols], in1=r_sb[h][g // 2][:, g % 2, cols], op=ALU.add)
+
+        def store(t):
+            h, g = tiles[t]
             nc.sync.dma_start(out=out[g, M_TILE * h : M_TILE * (h + 1), :], in_=res[t][:])
 
-        for pair in range(G // 2):
-            for i in range(2):
-                for g in (2 * pair, 2 * pair + 1):
-                    product(g, 0, i)
-
-        for t, (h, g) in enumerate(tiles):
+        def gate_and_multiply(t):
+            h, g = tiles[t]
             nc.scalar.activation(out=gate[t][:], in_=banks[g][0][:], func=ACT.Relu)
             if h + 1 < HALVES:
                 product(g, h + 1, 0)
             nc.vector.tensor_tensor(out=prod[t][:], in0=banks[g][1][:], in1=gate[t][:], op=ALU.mult)
             if h + 1 < HALVES:
                 product(g, h + 1, 1)
-            if t > 0:
-                finish(t - 1)
-        finish(len(tiles) - 1)
+
+        for g in range(G):
+            for i in range(2):
+                product(g, 0, i)
+
+        gate_and_multiply(0)
+        for t in range(0, len(tiles), 2):
+            split = POOL_COLS[t // 2]
+            add_residual(nc.gpsimd, t, slice(0, split))
+            for ahead in range(t + 1, min(t + 3, len(tiles))):
+                gate_and_multiply(ahead)
+            add_residual(nc.vector, t, slice(split, N))
+            store(t)
+            add_residual(nc.vector, t + 1, slice(0, N))
+            store(t + 1)

@@ -23,7 +23,7 @@ M_TILE = 128
 HALVES = M // M_TILE
 X_CHUNK = 256
 V_COLS = 168
-POOL_COLS = (384, 384, 384, 128)
+POOL_COLS = 384
 
 
 def tile_rows_gglu_relu_res_kernel(tc, x, w_words, w_scales, u_words, u_scales, r, out):
@@ -51,11 +51,10 @@ def tile_rows_gglu_relu_res_kernel(tc, x, w_words, w_scales, u_words, u_scales, 
         nc.vector.memset(scales[:].rearrange("p a m -> p (a m)").bitcast(I32), 0)
         nc.vector.memset(warm[:], 0.0)
         nc.scalar.activation(out=warm_act[:, 0:1], in_=warm[:, 0:1], func=ACT.Relu)
-        nc.gpsimd.tensor_tensor(out=warm_pool[:], in0=warm[:], in1=warm[:], op=ALU.add)
 
-        def load_scales(g):
+        def load_scales(queue, g):
             for i, src in enumerate((w_scales, u_scales)):
-                nc.sync.dma_start(out=scales[ROWS * g : ROWS * g + BLOCKS, i, :].bitcast(I32), in_=src[g].bitcast(I32))
+                queue.dma_start(out=scales[ROWS * g : ROWS * g + BLOCKS, i, :].bitcast(I32), in_=src[g].bitcast(I32))
 
         def load_r(h, q):
             nc.sync.dma_start(out=r_sb[h][q][:], in_=r_view[h, :, 2 * q : 2 * q + 2, :])
@@ -64,11 +63,12 @@ def tile_rows_gglu_relu_res_kernel(tc, x, w_words, w_scales, u_words, u_scales, 
             nc.sync.dma_start(out=x_raw[c][:], in_=x_rows[:, :, c * X_CHUNK : (c + 1) * X_CHUNK])
         for i, src in enumerate((w_words, u_words)):
             nc.sync.dma_start(out=words[i][:].bitcast(I32), in_=src.rearrange("g p b -> (g p) b").bitcast(I32))
-        load_scales(0)
-        load_scales(1)
+        load_scales(nc.gpsimd, 3)
+        nc.gpsimd.tensor_tensor(out=warm_pool[:], in0=warm[:], in1=warm[:], op=ALU.add)
+        load_scales(nc.sync, 0)
+        load_scales(nc.sync, 1)
         load_r(0, 0)
-        load_scales(2)
-        load_scales(3)
+        load_scales(nc.sync, 2)
         load_r(0, 1)
         load_r(1, 0)
         load_r(1, 1)
@@ -100,24 +100,30 @@ def tile_rows_gglu_relu_res_kernel(tc, x, w_words, w_scales, u_words, u_scales, 
         tiles = [(h, g) for h in range(HALVES) for g in range(G)]
         gate = [keep.tile([P, N], F32, name="gate%d" % t) for t in range(len(tiles))]
         prod = [keep.tile([P, N], F32, name="prod%d" % t) for t in range(len(tiles))]
+        last = len(tiles) - 1
         res = [
-            prod[t - 1] if t % 2 == 0 and t > 0 else keep.tile([P, N], F32, name="res%d" % t) for t in range(len(tiles))
+            prod[t - 1] if t in (2, 4) else keep.tile([P, N], F32, name="res%d" % t) for t in range(len(tiles))
         ]
+        whole = slice(0, N)
+        pool_cols, vector_cols = slice(0, POOL_COLS), slice(POOL_COLS, N)
+        halves = (slice(0, N // 2), slice(N // 2, N))
 
         def add_residual(engine, t, cols):
             h, g = tiles[t]
             engine.tensor_tensor(out=res[t][:, cols], in0=prod[t][:, cols], in1=r_sb[h][g // 2][:, g % 2, cols], op=ALU.add)
 
-        def store(t):
+        def store(t, cols):
             h, g = tiles[t]
-            nc.sync.dma_start(out=out[g, M_TILE * h : M_TILE * (h + 1), :], in_=res[t][:])
+            nc.sync.dma_start(out=out[g, M_TILE * h : M_TILE * (h + 1), cols], in_=res[t][:, cols])
 
-        def gate_and_multiply(t):
+        def gate_and_multiply(t, gate_parts, multiply_parts):
             h, g = tiles[t]
-            nc.scalar.activation(out=gate[t][:], in_=banks[g][0][:], func=ACT.Relu)
+            for cols in gate_parts:
+                nc.scalar.activation(out=gate[t][:, cols], in_=banks[g][0][:, cols], func=ACT.Relu)
             if h + 1 < HALVES:
                 product(g, h + 1, 0)
-            nc.vector.tensor_tensor(out=prod[t][:], in0=banks[g][1][:], in1=gate[t][:], op=ALU.mult)
+            for cols in multiply_parts:
+                nc.vector.tensor_tensor(out=prod[t][:, cols], in0=banks[g][1][:, cols], in1=gate[t][:, cols], op=ALU.mult)
             if h + 1 < HALVES:
                 product(g, h + 1, 1)
 
@@ -125,13 +131,18 @@ def tile_rows_gglu_relu_res_kernel(tc, x, w_words, w_scales, u_words, u_scales, 
             for i in range(2):
                 product(g, 0, i)
 
-        gate_and_multiply(0)
-        for t in range(0, len(tiles), 2):
-            split = POOL_COLS[t // 2]
-            add_residual(nc.gpsimd, t, slice(0, split))
-            for ahead in range(t + 1, min(t + 3, len(tiles))):
-                gate_and_multiply(ahead)
-            add_residual(nc.vector, t, slice(split, N))
-            store(t)
-            add_residual(nc.vector, t + 1, slice(0, N))
-            store(t + 1)
+        gate_and_multiply(0, (pool_cols, vector_cols), (pool_cols, vector_cols))
+        for t in range(0, last - 1, 2):
+            add_residual(nc.gpsimd, t, pool_cols)
+            gate_and_multiply(t + 1, (whole,), (whole,))
+            gate_and_multiply(t + 2, (whole,), (whole,))
+            adds = [(t + 1, whole), (t, vector_cols)]
+            for tile_index, cols in adds if t + 2 < last - 1 else reversed(adds):
+                add_residual(nc.vector, tile_index, cols)
+                store(tile_index, whole)
+        add_residual(nc.vector, last - 1, whole)
+        store(last - 1, whole)
+        gate_and_multiply(last, (whole,), halves)
+        for cols in halves:
+            add_residual(nc.vector, last, cols)
+            store(last, cols)

@@ -20,10 +20,8 @@ PACK = 4
 ROWS = D // PACK
 BLOCKS = D // 32
 M_TILE = 128
-HALVES = M // M_TILE
-X_CHUNK = 256
-V_COLS = 168
-POOL_COLS = 384
+HALF_N = N // 2
+VECTOR_CAST_COLS = (168, 192)
 
 
 def tile_rows_gglu_relu_res_kernel(tc, x, w_words, w_scales, u_words, u_scales, r, out):
@@ -33,12 +31,12 @@ def tile_rows_gglu_relu_res_kernel(tc, x, w_words, w_scales, u_words, u_scales, 
         psum = ctx.enter_context(tc.psum_pool(name="psum", bufs=1))
         ctx.enter_context(tc.manual_schedule())
 
-        chunks = N // X_CHUNK
+        left, right, whole = slice(0, HALF_N), slice(HALF_N, N), slice(0, N)
         x_rows = x.rearrange("g (p j) n -> (g p) j n", j=PACK)
-        x_raw = [keep.tile([P, PACK, X_CHUNK], F32, name="x_raw%d" % c) for c in range(chunks)]
-        x_bf = [keep.tile([P, X_CHUNK, PACK], BF16, name="x_bf%d" % c, align_bytes=256) for c in range(chunks)]
-        x_codes = keep.tile([P, N], U32, align_bytes=256)
-        x_scale = keep.tile([P, N], U8, align_bytes=256)
+        x_raw = [keep.tile([P, PACK, HALF_N], F32, name="x_raw%d" % c) for c in range(2)]
+        x_bf = [keep.tile([P, HALF_N, PACK], BF16, name="x_bf%d" % c, align_bytes=256) for c in range(2)]
+        x_codes = keep.tile([P, HALF_N + N], U32, align_bytes=256)
+        x_scale = keep.tile([P, HALF_N + N], U8, align_bytes=256)
         words = [keep.tile([P, 2 * M], U8, name="words%d" % i, align_bytes=256) for i in range(2)]
         scales = keep.tile([P, 2, M], U8, align_bytes=256)
         warm = keep.tile([P, 8], F32)
@@ -46,103 +44,125 @@ def tile_rows_gglu_relu_res_kernel(tc, x, w_words, w_scales, u_words, u_scales, 
         warm_pool = keep.tile([P, 8], F32)
         banks = [[psum.tile([M_TILE, N], F32, name="bank%d_%d" % (g, i)) for i in range(2)] for g in range(G)]
         r_view = r.rearrange("g (h p) n -> h p g n", p=M_TILE)
-        r_sb = [[keep.tile([P, 2, N], F32, name="r%d_%d" % (h, q)) for q in range(G // 2)] for h in range(HALVES)]
+        r_sb = [keep.tile([P, G, N], F32, name="r%d" % h) for h in range(2)]
+        gate = [keep.tile([P, G, N], F32, name="gate%d" % h) for h in range(2)]
+        prod = [keep.tile([P, G, N], F32, name="prod%d" % h) for h in range(2)]
+        res = [keep.tile([P, G, N], F32, name="res%d" % h) for h in range(2)]
 
         nc.vector.memset(scales[:].rearrange("p a m -> p (a m)").bitcast(I32), 0)
         nc.vector.memset(warm[:], 0.0)
+        nc.vector.memset(x_codes[:, left], 0)
+        nc.vector.memset(x_scale[:, left].bitcast(I32), 0)
         nc.scalar.activation(out=warm_act[:, 0:1], in_=warm[:, 0:1], func=ACT.Relu)
 
         def load_scales(queue, g):
             for i, src in enumerate((w_scales, u_scales)):
                 queue.dma_start(out=scales[ROWS * g : ROWS * g + BLOCKS, i, :].bitcast(I32), in_=src[g].bitcast(I32))
 
-        def load_r(h, q):
-            nc.sync.dma_start(out=r_sb[h][q][:], in_=r_view[h, :, 2 * q : 2 * q + 2, :])
+        def load_r(h, groups):
+            nc.sync.dma_start(out=r_sb[h][:, groups, :], in_=r_view[h, :, groups, :])
 
-        for c in range(chunks):
-            nc.sync.dma_start(out=x_raw[c][:], in_=x_rows[:, :, c * X_CHUNK : (c + 1) * X_CHUNK])
+        nc.sync.dma_start(out=x_raw[0][:], in_=x_rows[:, :, left])
         for i, src in enumerate((w_words, u_words)):
             nc.sync.dma_start(out=words[i][:].bitcast(I32), in_=src.rearrange("g p b -> (g p) b").bitcast(I32))
         load_scales(nc.gpsimd, 3)
         nc.gpsimd.tensor_tensor(out=warm_pool[:], in0=warm[:], in1=warm[:], op=ALU.add)
         load_scales(nc.sync, 0)
         load_scales(nc.sync, 1)
-        load_r(0, 0)
+        nc.sync.dma_start(out=x_raw[1][:], in_=x_rows[:, :, right])
         load_scales(nc.sync, 2)
-        load_r(0, 1)
-        load_r(1, 0)
-        load_r(1, 1)
+        for g in (1, 0, 2, 3):
+            load_r(0, slice(g, g + 1))
+        load_r(1, slice(0, 2))
+        load_r(1, slice(2, 4))
 
-        for c in range(chunks):
-            dst = x_bf[c][:].rearrange("p (a i) j -> p a j i", i=4)
-            src = x_raw[c][:].rearrange("p j (a i) -> p a j i", i=4)
-            nc.vector.tensor_copy(out=dst[:, : V_COLS // 4], in_=src[:, : V_COLS // 4])
-            nc.scalar.copy(out=dst[:, V_COLS // 4 :], in_=src[:, V_COLS // 4 :])
-            cols = slice(c * X_CHUNK, (c + 1) * X_CHUNK)
+        def interleave(copy, c, cols):
+            copy(
+                out=x_bf[c][:, cols, :].rearrange("p (a i) j -> p a j i", i=4),
+                in_=x_raw[c][:, :, cols].rearrange("p j (a i) -> p a j i", i=4),
+            )
+
+        def quantise(c):
+            cols = slice((c + 1) * HALF_N, (c + 2) * HALF_N)
             nc.vector.quantize_mx(
                 out=x_codes[:, cols].bitcast(FP8X4),
                 scales=x_scale[:, cols],
                 in_=x_bf[c][:].rearrange("p n j -> p (n j)"),
             )
 
-        def product(g, h, i):
-            rows = slice(ROWS * g, ROWS * (g + 1))
-            nc.tensor.matmul_mx(
-                out=banks[g][i][:],
-                lhsT=words[i][rows, 2 * M_TILE * h : 2 * M_TILE * (h + 1)].bitcast(FP4X4),
-                lhsT_scale=scales[rows, i, M_TILE * h : M_TILE * (h + 1)],
-                rhs=x_codes[rows, :].bitcast(FP8X4),
-                rhs_scale=x_scale[rows, :],
-                start=True,
-                stop=True,
+        def products(groups, h, first):
+            for i in range(2):
+                for g in groups:
+                    rows = slice(ROWS * g, ROWS * (g + 1))
+                    nc.tensor.matmul_mx(
+                        out=banks[g][i][:],
+                        lhsT=words[i][rows, 2 * M_TILE * h : 2 * M_TILE * (h + 1)].bitcast(FP4X4),
+                        lhsT_scale=scales[rows, i, M_TILE * h : M_TILE * (h + 1)],
+                        rhs=x_codes[rows, first : first + N].bitcast(FP8X4),
+                        rhs_scale=x_scale[rows, first : first + N],
+                        start=True,
+                        stop=True,
+                    )
+
+        def relu(h, g, bank_cols, cols):
+            nc.scalar.activation(out=gate[h][:, g, cols], in_=banks[g][0][:, bank_cols], func=ACT.Relu)
+
+        def multiply(h, g, bank_cols, cols):
+            nc.vector.tensor_tensor(
+                out=prod[h][:, g, cols], in0=banks[g][1][:, bank_cols], in1=gate[h][:, g, cols], op=ALU.mult
             )
 
-        tiles = [(h, g) for h in range(HALVES) for g in range(G)]
-        gate = [keep.tile([P, N], F32, name="gate%d" % t) for t in range(len(tiles))]
-        prod = [keep.tile([P, N], F32, name="prod%d" % t) for t in range(len(tiles))]
-        last = len(tiles) - 1
-        res = [
-            prod[t - 1] if t in (2, 4) else keep.tile([P, N], F32, name="res%d" % t) for t in range(len(tiles))
-        ]
-        whole = slice(0, N)
-        pool_cols, vector_cols = slice(0, POOL_COLS), slice(POOL_COLS, N)
-        halves = (slice(0, N // 2), slice(N // 2, N))
+        def gated(h, groups, bank_cols, cols):
+            for g in groups:
+                relu(h, g, bank_cols, cols)
+                multiply(h, g, bank_cols, cols)
 
-        def add_residual(engine, t, cols):
-            h, g = tiles[t]
-            engine.tensor_tensor(out=res[t][:, cols], in0=prod[t][:, cols], in1=r_sb[h][g // 2][:, g % 2, cols], op=ALU.add)
+        def add_residual(engine, h, groups, cols):
+            engine.tensor_tensor(
+                out=res[h][:, groups, cols], in0=prod[h][:, groups, cols], in1=r_sb[h][:, groups, cols], op=ALU.add
+            )
 
-        def store(t, cols):
-            h, g = tiles[t]
-            nc.sync.dma_start(out=out[g, M_TILE * h : M_TILE * (h + 1), cols], in_=res[t][:, cols])
+        def store(h, g):
+            nc.sync.dma_start(out=out[g, M_TILE * h : M_TILE * (h + 1), :], in_=res[h][:, g, :])
 
-        def gate_and_multiply(t, gate_parts, multiply_parts):
-            h, g = tiles[t]
-            for cols in gate_parts:
-                nc.scalar.activation(out=gate[t][:, cols], in_=banks[g][0][:, cols], func=ACT.Relu)
-            if h + 1 < HALVES:
-                product(g, h + 1, 0)
-            for cols in multiply_parts:
-                nc.vector.tensor_tensor(out=prod[t][:, cols], in0=banks[g][1][:, cols], in1=gate[t][:, cols], op=ALU.mult)
-            if h + 1 < HALVES:
-                product(g, h + 1, 1)
+        vector_cols = [slice(0, split) for split in VECTOR_CAST_COLS]
+        scalar_cols = [slice(split, HALF_N) for split in VECTOR_CAST_COLS]
+        interleave(nc.vector.tensor_copy, 0, vector_cols[0])
+        interleave(nc.scalar.copy, 0, scalar_cols[0])
+        quantise(0)
+        products((0, 1), 0, 0)
+        products((2, 3), 0, 0)
 
-        for g in range(G):
-            for i in range(2):
-                product(g, 0, i)
+        interleave(nc.vector.tensor_copy, 1, vector_cols[1])
+        gated(0, (0, 1), right, left)
+        interleave(nc.scalar.copy, 1, scalar_cols[1])
+        quantise(1)
+        products((0, 1), 0, HALF_N)
+        add_residual(nc.gpsimd, 0, slice(1, 2), left)
+        gated(0, (2, 3), right, left)
+        products((2, 3), 0, HALF_N)
+        add_residual(nc.vector, 0, slice(0, 3, 2), left)
 
-        gate_and_multiply(0, (pool_cols, vector_cols), (pool_cols, vector_cols))
-        for t in range(0, last - 1, 2):
-            add_residual(nc.gpsimd, t, pool_cols)
-            gate_and_multiply(t + 1, (whole,), (whole,))
-            gate_and_multiply(t + 2, (whole,), (whole,))
-            adds = [(t + 1, whole), (t, vector_cols)]
-            for tile_index, cols in adds if t + 2 < last - 1 else reversed(adds):
-                add_residual(nc.vector, tile_index, cols)
-                store(tile_index, whole)
-        add_residual(nc.vector, last - 1, whole)
-        store(last - 1, whole)
-        gate_and_multiply(last, (whole,), halves)
-        for cols in halves:
-            add_residual(nc.vector, last, cols)
-            store(last, cols)
+        add_residual(nc.gpsimd, 0, slice(3, 4), left)
+        gated(0, (0, 1), right, right)
+        products((0, 1), 1, HALF_N)
+        add_residual(nc.gpsimd, 0, slice(0, 1), right)
+        store(0, 0)
+        gated(0, (2, 3), right, right)
+        products((2, 3), 1, HALF_N)
+        add_residual(nc.vector, 0, slice(1, 2), right)
+        store(0, 1)
+
+        add_residual(nc.gpsimd, 0, slice(2, 4), right)
+        store(0, 2)
+        store(0, 3)
+        gated(1, (0, 1), whole, whole)
+        add_residual(nc.vector, 1, slice(0, 1), whole)
+        store(1, 0)
+
+        add_residual(nc.gpsimd, 1, slice(1, 2), whole)
+        store(1, 1)
+        gated(1, (2, 3), whole, whole)
+        for g in (2, 3):
+            add_residual(nc.vector, 1, slice(g, g + 1), whole)
+            store(1, g)

from contextlib import ExitStack

import concourse.mybir as mybir

G, D, M, N = 4, 128, 256, 512
FLOPS = 2 * 2 * G * D * M * N

F32 = mybir.dt.float32
BF16 = mybir.dt.bfloat16
I32 = mybir.dt.int32
U32 = mybir.dt.uint32
U8 = mybir.dt.uint8
FP8X4 = mybir.dt.float8_e4m3fn_x4
FP4X4 = mybir.dt.float4_e2m1fn_x4
ALU = mybir.AluOpType
ACT = mybir.ActivationFunctionType

P = 128
PACK = 4
ROWS = D // PACK
BLOCKS = D // 32
M_TILE = 128
HALF_N = N // 2
VECTOR_CAST_COLS = (168, 192)


def tile_rows_gglu_relu_res_kernel(tc, x, w_words, w_scales, u_words, u_scales, r, out):
    nc = tc.nc
    with ExitStack() as ctx:
        keep = ctx.enter_context(tc.tile_pool(name="keep", bufs=1))
        psum = ctx.enter_context(tc.psum_pool(name="psum", bufs=1))
        ctx.enter_context(tc.manual_schedule())

        left, right, whole = slice(0, HALF_N), slice(HALF_N, N), slice(0, N)
        x_rows = x.rearrange("g (p j) n -> (g p) j n", j=PACK)
        x_raw = [keep.tile([P, PACK, HALF_N], F32, name="x_raw%d" % c) for c in range(2)]
        x_bf = [keep.tile([P, HALF_N, PACK], BF16, name="x_bf%d" % c, align_bytes=256) for c in range(2)]
        x_codes = keep.tile([P, HALF_N + N], U32, align_bytes=256)
        x_scale = keep.tile([P, HALF_N + N], U8, align_bytes=256)
        words = [keep.tile([P, 2 * M], U8, name="words%d" % i, align_bytes=256) for i in range(2)]
        scales = keep.tile([P, 2, M], U8, align_bytes=256)
        warm = keep.tile([P, 8], F32)
        warm_act = keep.tile([P, 8], F32)
        warm_pool = keep.tile([P, 8], F32)
        banks = [[psum.tile([M_TILE, N], F32, name="bank%d_%d" % (g, i)) for i in range(2)] for g in range(G)]
        r_view = r.rearrange("g (h p) n -> h p g n", p=M_TILE)
        r_sb = [keep.tile([P, G, N], F32, name="r%d" % h) for h in range(2)]
        gate = [keep.tile([P, G, N], F32, name="gate%d" % h) for h in range(2)]
        prod = [keep.tile([P, G, N], F32, name="prod%d" % h) for h in range(2)]
        res = [keep.tile([P, G, N], F32, name="res%d" % h) for h in range(2)]

        nc.vector.memset(scales[:].rearrange("p a m -> p (a m)").bitcast(I32), 0)
        nc.vector.memset(warm[:], 0.0)
        nc.vector.memset(x_codes[:, left], 0)
        nc.vector.memset(x_scale[:, left].bitcast(I32), 0)
        nc.scalar.activation(out=warm_act[:, 0:1], in_=warm[:, 0:1], func=ACT.Relu)

        def load_scales(queue, g):
            for i, src in enumerate((w_scales, u_scales)):
                queue.dma_start(out=scales[ROWS * g : ROWS * g + BLOCKS, i, :].bitcast(I32), in_=src[g].bitcast(I32))

        def load_r(h, groups):
            nc.sync.dma_start(out=r_sb[h][:, groups, :], in_=r_view[h, :, groups, :])

        nc.sync.dma_start(out=x_raw[0][:], in_=x_rows[:, :, left])
        for i, src in enumerate((w_words, u_words)):
            nc.sync.dma_start(out=words[i][:].bitcast(I32), in_=src.rearrange("g p b -> (g p) b").bitcast(I32))
        load_scales(nc.gpsimd, 3)
        nc.gpsimd.tensor_tensor(out=warm_pool[:], in0=warm[:], in1=warm[:], op=ALU.add)
        load_scales(nc.sync, 0)
        load_scales(nc.sync, 1)
        nc.sync.dma_start(out=x_raw[1][:], in_=x_rows[:, :, right])
        load_scales(nc.sync, 2)
        for g in (1, 0, 2, 3):
            load_r(0, slice(g, g + 1))
        load_r(1, slice(0, 2))
        load_r(1, slice(2, 4))

        def interleave(copy, c, cols):
            copy(
                out=x_bf[c][:, cols, :].rearrange("p (a i) j -> p a j i", i=4),
                in_=x_raw[c][:, :, cols].rearrange("p j (a i) -> p a j i", i=4),
            )

        def quantise(c):
            cols = slice((c + 1) * HALF_N, (c + 2) * HALF_N)
            nc.vector.quantize_mx(
                out=x_codes[:, cols].bitcast(FP8X4),
                scales=x_scale[:, cols],
                in_=x_bf[c][:].rearrange("p n j -> p (n j)"),
            )

        def products(groups, h, first):
            for i in range(2):
                for g in groups:
                    rows = slice(ROWS * g, ROWS * (g + 1))
                    nc.tensor.matmul_mx(
                        out=banks[g][i][:],
                        lhsT=words[i][rows, 2 * M_TILE * h : 2 * M_TILE * (h + 1)].bitcast(FP4X4),
                        lhsT_scale=scales[rows, i, M_TILE * h : M_TILE * (h + 1)],
                        rhs=x_codes[rows, first : first + N].bitcast(FP8X4),
                        rhs_scale=x_scale[rows, first : first + N],
                        start=True,
                        stop=True,
                    )

        def relu(h, g, bank_cols, cols):
            nc.scalar.activation(out=gate[h][:, g, cols], in_=banks[g][0][:, bank_cols], func=ACT.Relu)

        def multiply(h, g, bank_cols, cols):
            nc.vector.tensor_tensor(
                out=prod[h][:, g, cols], in0=banks[g][1][:, bank_cols], in1=gate[h][:, g, cols], op=ALU.mult
            )

        def gated(h, groups, bank_cols, cols):
            for g in groups:
                relu(h, g, bank_cols, cols)
                multiply(h, g, bank_cols, cols)

        def add_residual(engine, h, groups, cols):
            engine.tensor_tensor(
                out=res[h][:, groups, cols], in0=prod[h][:, groups, cols], in1=r_sb[h][:, groups, cols], op=ALU.add
            )

        def store(h, g):
            nc.sync.dma_start(out=out[g, M_TILE * h : M_TILE * (h + 1), :], in_=res[h][:, g, :])

        vector_cols = [slice(0, split) for split in VECTOR_CAST_COLS]
        scalar_cols = [slice(split, HALF_N) for split in VECTOR_CAST_COLS]
        interleave(nc.vector.tensor_copy, 0, vector_cols[0])
        interleave(nc.scalar.copy, 0, scalar_cols[0])
        quantise(0)
        products((0, 1), 0, 0)
        products((2, 3), 0, 0)

        interleave(nc.vector.tensor_copy, 1, vector_cols[1])
        gated(0, (0, 1), right, left)
        interleave(nc.scalar.copy, 1, scalar_cols[1])
        quantise(1)
        products((0, 1), 0, HALF_N)
        add_residual(nc.gpsimd, 0, slice(1, 2), left)
        gated(0, (2, 3), right, left)
        products((2, 3), 0, HALF_N)
        add_residual(nc.vector, 0, slice(0, 3, 2), left)

        add_residual(nc.gpsimd, 0, slice(3, 4), left)
        gated(0, (0, 1), right, right)
        products((0, 1), 1, HALF_N)
        add_residual(nc.gpsimd, 0, slice(0, 1), right)
        store(0, 0)
        gated(0, (2, 3), right, right)
        products((2, 3), 1, HALF_N)
        add_residual(nc.vector, 0, slice(1, 2), right)
        store(0, 1)

        add_residual(nc.gpsimd, 0, slice(2, 4), right)
        store(0, 2)
        store(0, 3)
        gated(1, (0, 1), whole, whole)
        add_residual(nc.vector, 1, slice(0, 1), whole)
        store(1, 0)

        add_residual(nc.gpsimd, 1, slice(1, 2), whole)
        store(1, 1)
        gated(1, (2, 3), whole, whole)
        for g in (2, 3):
            add_residual(nc.vector, 1, slice(g, g + 1), whole)
            store(1, g)
